import numpy as np, ml_dtypes
CORES = [122,123,126,250,251,254,378,379,382,506,507,510]
N = 12
T = 2048
def entries(a): return a.T.reshape(-1)
def pack(v, P): return np.ascontiguousarray(np.asarray(v, np.int32).reshape(-1, P).T)
def lists(rng, how):
    h = rng.integers(0, N * T, 8)
    if how == "zero": h[:] = 0
    if how == "blocks": h = T * rng.integers(1, N, 8)
    if how == "last": h[:] = N * T - 1
    if how == "mixed": h = T * rng.choice([q for q in range(N) if q & (q - 1)], 8) + rng.integers(1, T, 8)
    if how == "small": h = rng.integers(1, T, 8)
    h[1:] = 0
    return {"hh": np.broadcast_to(pack(np.concatenate([h, np.zeros(24, np.int64)]), 16), (N, 16, 2)).copy()}
def setup_inputs(rng):
    return dict({"x": rng.standard_normal((N, 128, T), dtype=np.float32).astype(ml_dtypes.bfloat16)}, **lists(rng, "uniform"))
def setup_inputs_blocks(rng):
    d = setup_inputs(rng); d.update(lists(rng, "blocks"))
    for k in ("x",): d[k] = (d[k].astype(np.float32) * 1048576.0).astype(d[k].dtype)
    return d
def setup_inputs_last(rng):
    d = setup_inputs(rng); d.update(lists(rng, "last"))
    for k in ("x",): d[k] = (d[k].astype(np.float32) * (1 / 1024.0)).astype(d[k].dtype)
    return d
def setup_inputs_mixed(rng):
    d = setup_inputs(rng); d.update(lists(rng, "mixed"))
    return d
def setup_inputs_small(rng):
    d = setup_inputs(rng); d.update(lists(rng, "small"))
    return d
def setup_inputs_zero(rng):
    d = setup_inputs(rng); d.update(lists(rng, "zero"))
    return d
def check_inputs(x):
    bad = []
    if x["hh"].min() < 0 or x["hh"].max() >= N * T: bad.append("hh out of range")
    if entries(x["hh"][0])[1:].any(): bad.append("an entry that should be 0 isn't")
    if not all(np.array_equal(a, x["hh"][0]) for a in x["hh"]): bad.append("hh isn't alike on all ranks")
    return bad
def reference(x, hh):
    h = entries(hh[0]); A = np.concatenate(list(x), axis=1)
    Y = np.roll(A, -int(h[0]), axis=1)
    return {"y": np.stack([Y[:, T * r:T * r + T] for r in range(N)])}

@@ -1,0 +1,209 @@
+from concourse.bass import DstId, RemoteDMATransfer
+from concourse.mybir import AluOpType as Op, ActivationFunctionType as Act
+
+WORLD = 512
+N, W = 12, 2048
+K = 8
+C = W // K
+
+SCRATCH = {
+    "xs": ("sbuf", [128, W], "bfloat16"),
+    "rot": ("sbuf", [128, W], "bfloat16"),
+    "tab": ("sbuf", [128, N * C], "bfloat16"),
+    "sel": ("sbuf", [128, 3 * C], "bfloat16"),
+    "fin": ("sbuf", [128, W], "bfloat16"),
+    "hrow": ("sbuf", [1, 2], "int32"),
+    "hb": ("sbuf", [128, 2], "int32"),
+    "hf": ("sbuf", [128, 1], "float32"),
+    "hd": ("dram", [128, 2], "int32"),
+    "pi": ("sbuf", [128, 1], "int32"),
+    "pg": ("sbuf", [128, 1], "int32"),
+    "pf": ("sbuf", [128, 1], "float32"),
+    "ja": ("sbuf", [128, W // 16], "int32"),
+    "jb": ("sbuf", [128, W // 16], "int32"),
+    "jc": ("sbuf", [128, W // 16], "int32"),
+    "jd": ("sbuf", [128, W // 16], "int32"),
+    "off1": ("sbuf", [128, W // 16], "uint16"),
+    "ba": ("sbuf", [128, 3 * C // 16], "int32"),
+    "bb": ("sbuf", [128, 3 * C // 16], "int32"),
+    "ta": ("sbuf", [128, 3 * C // 16], "int32"),
+    "tb": ("sbuf", [128, 3 * C // 16], "int32"),
+    "q0": ("sbuf", [128, 3 * C // 16], "int32"),
+    "q1": ("sbuf", [128, 3 * C // 16], "int32"),
+    "q2": ("sbuf", [128, 3 * C // 16], "int32"),
+    "q3": ("sbuf", [128, 3 * C // 16], "int32"),
+    "q4": ("sbuf", [128, 3 * C // 16], "int32"),
+    "q5": ("sbuf", [128, 3 * C // 16], "int32"),
+    "off2": ("sbuf", [128, 3 * C // 16], "uint16"),
+}
+SEMAPHORES = ["xl", "hl", "hs", "hr", "gi", "gb", "v", "l1", "l2", "ra", "rb", "ro", "s1a", "s1b", "ca", "cb", "sw",
+              "sl", "so", "fin0", "fin1", "st", "loc"]
+
+
+def bits(m):
+    return [1 << i for i in range(16) if (m >> i) & 1]
+
+
+def rank_program(g, core, T, topo):
+    sem = T.sem
+    place = lambda c: (topo.host(c), topo.chip(c))
+    if place(core) not in [place(c) for c in T.cores]:
+        return
+    chip = [c for c in range(WORLD) if place(c) == place(core)]
+    me = chip.index(core)
+    ranks = [r for r in range(N) if place(T.cores[r]) == place(core)]
+    r0 = ranks[0]
+    mine = T.rank_of(core)
+    pos = None if mine is None else mine - r0
+    group = [c for c in range(WORLD) if place(c) in [place(d) for d in T.cores] and place(c) != place(core)]
+    twins = [c for c in group if topo.may_write(core, c)
+             and [d for d in range(WORLD) if place(d) == place(c)].index(c) == me]
+    sw = [c for c in twins if topo.same_plane(core, c)][0]
+    cab = [c for c in twins if topo.rack(topo.host(c)) != topo.rack(topo.host(core))][0]
+    first_rank = lambda c: [r for r in range(N) if place(T.cores[r]) == place(c)][0]
+    on = bits(topo.mask(core, chip[(me + 1) % K]))
+    off = bits(topo.mask(core, cab) & topo.mask(core, sw))
+    m_sw, m_cab = off[0::2], off[1::2]
+    dst = lambda d: DstId(rid=topo.addr(d, core)[0], pnc=topo.addr(d, core)[1])
+    nloc = [0]
+
+    def send(ts):
+        for t in ts:
+            nloc[0] += len(t[4])
+        g.remote_dma_fused([RemoteDMATransfer(dst_ids=[dst(d)], dma_engine_mask=sum(e), remote_sem=s, src=i, dst=o)
+                            for d, o, i, s, e in ts], local_sem=sem.loc)
+
+    if mine is not None:
+        g.scalar.dma_start(out=T.hrow[0:1, 0:2], in_=T.hh[0:1, 0:2]).then_inc(sem.hl, 16)
+        g.sync.dma_start(out=T.xs[:], in_=T.x[:]).then_inc(sem.xl, 16)
+
+    g.iota(T.pi[:], [[0, 1]], 0, 1).then_inc(sem.gi, 1)
+    if mine is not None:
+        g.iota(T.ja[:], [[16, W // 16]], 0, 1).then_inc(sem.gi, 1)
+    g.iota(T.ba[:], [[W, 3], [16, C // 16]], W * r0 + C * me, 1).then_inc(sem.gi, 1)
+    g.iota(T.ta[:], [[0, 3], [16, C // 16]], 0, 1).then_inc(sem.gi, 1)
+    g.vector.wait_ge(sem.gi, 3 if mine is None else 4)
+    nv = [0]
+
+    def vec(call, *a):
+        call(*a).then_inc(sem.v, 1)
+        nv[0] += 1
+        g.vector.wait_ge(sem.v, nv[0])
+
+    vec(g.vector.tensor_scalar, T.pg[:], T.pi[:], 112, None, Op.bitwise_and)
+    vec(g.vector.tensor_copy, T.pf[:], T.pg[:])
+    if mine is not None:
+        vec(g.vector.tensor_scalar, T.jb[:], T.ja[:], T.pf[:, 0:1], None, Op.subtract)
+    vec(g.vector.tensor_scalar, T.bb[:], T.ba[:], T.pf[:, 0:1], None, Op.subtract)
+    vec(g.vector.tensor_scalar, T.tb[:], T.ta[:], T.pf[:, 0:1], None, Op.subtract)
+
+    helpers = [c for c in chip if T.rank_of(c) is None]
+    h_sender = T.cores[ranks[-1]]
+    if mine is not None:
+        g.wait_ge(sem.hl, 16)
+        g.partition_broadcast(T.hb[:], T.hrow[0:1, 0:2], 128).then_inc(sem.gb, 1)
+        g.vector.wait_ge(sem.gb, 1)
+        if core == h_sender:
+            g.sync.wait_ge(sem.gb, 1)
+            g.sync.dma_start(out=T.hd[:], in_=T.hb[:]).then_inc(sem.hs, 16)
+    else:
+        g.sync.wait_ge(sem.hr, 1)
+        g.sync.dma_start(out=T.hb[:], in_=T.hd[:]).then_inc(sem.hl, 16)
+        g.vector.wait_ge(sem.hl, 16)
+    vec(g.vector.tensor_copy, T.hf[:], T.hb[:, 0:1])
+
+    mycols = lambda r: (r * C, r * C + C)
+    if mine is not None:
+        vec(g.vector.tensor_scalar, T.jc[:], T.jb[:], T.hf[:, 0:1], None, Op.add)
+        vec(g.vector.tensor_scalar, T.jd[:], T.jc[:], W - 1, None, Op.bitwise_and)
+        g.vector.tensor_copy(T.off1[:], T.jd[:]).then_inc(sem.l1, 1)
+        for q in (g.vector, g.scalar):
+            q.wait_ge(sem.l1, 1)
+            q.wait_ge(sem.xl, 16)
+        waves = [list(range(0, K, 2)), list(range(1, K, 2))]
+        a0, a1 = mycols(mine)
+        for n, k in enumerate(waves[0] + waves[1]):
+            out = T.tab[:, a0:a1] if k == me else T.rot[:, k * C:k * C + C]
+            s = sem.ro if k == me else sem.ra if k in waves[0] else sem.rb
+            src = T.xs[:, 0:W].indirect(T.off1[:, k * C // 16:(k + 1) * C // 16])
+            if n % 2 == 0:
+                g.vector.tensor_copy(out, src).then_inc(s, 1)
+            else:
+                g.scalar.activation(out, src, Act.Copy).then_inc(s, 1)
+        for w, s in zip(waves, (sem.ra, sem.rb)):
+            ks = [k for k in w if k != me]
+            g.wait_ge(s, len(ks))
+            send([(chip[k], T.tab[:, a0:a1], T.rot[:, k * C:k * C + C], sem.s1b if pos == 2 else sem.s1a, on[n::4])
+                  for n, k in enumerate(ks)])
+        g.wait_ge(sem.ro, 1)
+
+    per = len(on[0::4])
+    base = r0 * C
+    chunks = [(0, 2 * C, sem.s1a, sem.ca, per * len([i for i in (0, 1) if i != pos])),
+              (2 * C, 3 * C, sem.s1b, sem.cb, per * len([i for i in (2,) if i != pos]))]
+    for lo, hi, s_in, s_out, n in chunks:
+        if n:
+            g.wait_ge(s_in, n)
+        ap = T.tab[:, base + lo:base + hi]
+        send([(cab, ap, ap, s_out, m_cab), (sw, ap, ap, sem.sw, m_sw)])
+    if core == h_sender:
+        g.wait_ge(sem.hs, 16)
+        e = m_sw[0]
+        nloc[0] += 1
+        g.remote_dma_fused([RemoteDMATransfer(dst_ids=[dst(c) for c in helpers], dma_engine_mask=e, remote_sem=sem.hr,
+                                              srcs=[T.hd[:]], dsts=[T.hd[:] for c in helpers])], local_sem=sem.loc)
+    cbase = first_rank(cab) * C
+    relay = [m_sw, off]
+    for (lo, hi, s_in, s_out, n), e in zip(chunks, relay):
+        g.wait_ge(s_out, len(m_cab))
+        ap = T.tab[:, cbase + lo:cbase + hi]
+        send([(sw, ap, ap, sem.sw, e)])
+
+    vec(g.vector.tensor_scalar, T.q0[:], T.bb[:], T.hf[:, 0:1], None, Op.add)
+    vec(g.vector.tensor_scalar, T.q1[:], T.q0[:], 11, None, Op.arith_shift_right)
+    vec(g.vector.tensor_scalar, T.q2[:], T.q1[:], N, -N * C, Op.is_ge, Op.mult)
+    vec(g.vector.tensor_scalar, T.q3[:], T.q1[:], C, None, Op.mult)
+    vec(g.vector.tensor_tensor, T.q4[:], T.q3[:], T.q2[:], Op.add)
+    vec(g.vector.tensor_tensor, T.q5[:], T.q4[:], T.tb[:], Op.add)
+    g.vector.tensor_copy(T.off2[:], T.q5[:]).then_inc(sem.l2, 1)
+    nsw = 2 * len(m_sw) + len(relay[0]) + len(relay[1])
+    for q in (g.vector, g.scalar):
+        q.wait_ge(sem.l2, 1)
+        q.wait_ge(sem.sw, nsw)
+        q.wait_ge(sem.ca, len(m_cab))
+        q.wait_ge(sem.cb, len(m_cab))
+        if mine is not None:
+            q.wait_ge(sem.ro, 1)
+        for lo, hi, s_in, s_out, n in chunks:
+            if n:
+                q.wait_ge(s_in, n)
+
+    def pick(q, i, lo, hi):
+        out, s = (T.fin[:, me * C + lo:me * C + hi], sem.so) if i == pos else (T.sel[:, i * C + lo:i * C + hi], sem.sl)
+        src = T.tab[:, 0:N * C].indirect(T.off2[:, (i * C + lo) // 16:(i * C + hi) // 16])
+        if q == 0:
+            g.vector.tensor_copy(out, src).then_inc(s, 1)
+        else:
+            g.scalar.activation(out, src, Act.Copy).then_inc(s, 1)
+
+    mid = 1 if pos is None else pos
+    ends = [i for i in range(3) if i != mid]
+    for q in (0, 1):
+        pick(q, ends[q], 0, C)
+        pick(q, mid, q * C // 2, (q + 1) * C // 2)
+    targets = [i for i in range(3) if i != pos]
+    g.wait_ge(sem.sl, 4 if pos is None else 2)
+    fe = lambda k: 2 if T.rank_of(chip[k]) is None else 4
+    send([(T.cores[r0 + i], T.fin[:, me * C:me * C + C], T.sel[:, i * C:i * C + C], sem.fin0 if me < K // 2 else sem.fin1,
+           off[n * fe(me):(n + 1) * fe(me)]) for n, i in enumerate(targets)])
+
+    if mine is not None:
+        for half, (q, s) in enumerate(((g.sync, sem.fin0), (g.scalar, sem.fin1))):
+            ks = list(range(half * K // 2, (half + 1) * K // 2))
+            q.wait_ge(s, sum([fe(k) for k in ks if k != me]))
+            if me in ks:
+                q.wait_ge(sem.so, 2)
+            q.dma_start(out=T.y[:, half * W // 2:(half + 1) * W // 2],
+                        in_=T.fin[:, half * W // 2:(half + 1) * W // 2]).then_inc(sem.st, 16)
+        g.wait_ge(sem.st, 32)
+    g.wait_ge(sem.loc, nloc[0])

@@ -5,6 +5,7 @@ WORLD = 512
 N, W = 12, 2048
 K = 8
 C = W // K
+L1, L2 = W // 16, 3 * C // 16
 
 SCRATCH = {
     "xs": ("sbuf", [128, W], "bfloat16"),
@@ -15,28 +16,27 @@ SCRATCH = {
     "hrow": ("sbuf", [1, 2], "int32"),
     "hb": ("sbuf", [128, 2], "int32"),
     "hf": ("sbuf", [128, 1], "float32"),
-    "hd": ("dram", [128, 2], "int32"),
     "pi": ("sbuf", [128, 1], "int32"),
     "pg": ("sbuf", [128, 1], "int32"),
     "pf": ("sbuf", [128, 1], "float32"),
-    "ja": ("sbuf", [128, W // 16], "int32"),
-    "jb": ("sbuf", [128, W // 16], "int32"),
-    "jc": ("sbuf", [128, W // 16], "int32"),
-    "jd": ("sbuf", [128, W // 16], "int32"),
-    "off1": ("sbuf", [128, W // 16], "uint16"),
-    "ba": ("sbuf", [128, 3 * C // 16], "int32"),
-    "bb": ("sbuf", [128, 3 * C // 16], "int32"),
-    "ta": ("sbuf", [128, 3 * C // 16], "int32"),
-    "tb": ("sbuf", [128, 3 * C // 16], "int32"),
-    "q0": ("sbuf", [128, 3 * C // 16], "int32"),
-    "q1": ("sbuf", [128, 3 * C // 16], "int32"),
-    "q2": ("sbuf", [128, 3 * C // 16], "int32"),
-    "q3": ("sbuf", [128, 3 * C // 16], "int32"),
-    "q4": ("sbuf", [128, 3 * C // 16], "int32"),
-    "q5": ("sbuf", [128, 3 * C // 16], "int32"),
-    "off2": ("sbuf", [128, 3 * C // 16], "uint16"),
+    "ja": ("sbuf", [128, L1], "int32"),
+    "jb": ("sbuf", [128, L1], "int32"),
+    "jc": ("sbuf", [128, L1], "int32"),
+    "jd": ("sbuf", [128, L1], "int32"),
+    "off1": ("sbuf", [128, L1], "uint16"),
+    "ba": ("sbuf", [128, L2], "int32"),
+    "bb": ("sbuf", [128, L2], "int32"),
+    "ta": ("sbuf", [128, L2], "int32"),
+    "tb": ("sbuf", [128, L2], "int32"),
+    "q0": ("sbuf", [128, L2], "int32"),
+    "q1": ("sbuf", [128, L2], "int32"),
+    "q2": ("sbuf", [128, L2], "int32"),
+    "q3": ("sbuf", [128, L2], "int32"),
+    "q4": ("sbuf", [128, L2], "int32"),
+    "q5": ("sbuf", [128, L2], "int32"),
+    "off2": ("sbuf", [128, L2], "uint16"),
 }
-SEMAPHORES = ["xl", "hl", "hs", "hr", "gi", "gb", "v", "l1", "l2", "ra", "rb", "ro", "s1a", "s1b", "ca", "cb", "sw",
+SEMAPHORES = ["xl", "hl", "hr", "gi", "gb", "v", "l1", "l2", "ra", "rb", "ro", "s1a", "s1b", "ca", "cb", "sw",
               "sl", "so", "fin0", "fin1", "st", "loc"]
 
 
@@ -49,29 +49,35 @@ def rank_program(g, core, T, topo):
     place = lambda c: (topo.host(c), topo.chip(c))
     if place(core) not in [place(c) for c in T.cores]:
         return
-    chip = [c for c in range(WORLD) if place(c) == place(core)]
+    on_chip = lambda c: [d for d in range(WORLD) if place(d) == place(c)]
+
+    def order(cs):
+        a, b = [[c for c in cs if topo.die(c) == topo.die(e)] for e in (cs[0], cs[-1])]
+        return [c for i in (0, 2, 1, 3) for c in (a[i], b[i])]
+
+    chip = order(on_chip(core))
     me = chip.index(core)
-    ranks = [r for r in range(N) if place(T.cores[r]) == place(core)]
+    other = [d for d in T.cores if place(d) != place(core)]
+    sw_chip = order(on_chip([d for d in other if topo.same_plane(core, d)][0]))
+    cab_chip = order(on_chip([d for d in other if topo.rack(topo.host(d)) != topo.rack(topo.host(core))
+                              and topo.may_write(core, d)][0]))
+    sw, cab = sw_chip[me], cab_chip[me]
+    ranks_at = lambda cs: sorted([T.rank_of(c) for c in cs if T.rank_of(c) is not None])
+    ranks = ranks_at(chip)
     r0 = ranks[0]
     mine = T.rank_of(core)
     pos = None if mine is None else mine - r0
-    group = [c for c in range(WORLD) if place(c) in [place(d) for d in T.cores] and place(c) != place(core)]
-    twins = [c for c in group if topo.may_write(core, c)
-             and [d for d in range(WORLD) if place(d) == place(c)].index(c) == me]
-    sw = [c for c in twins if topo.same_plane(core, c)][0]
-    cab = [c for c in twins if topo.rack(topo.host(c)) != topo.rack(topo.host(core))][0]
-    first_rank = lambda c: [r for r in range(N) if place(T.cores[r]) == place(c)][0]
     on = bits(topo.mask(core, chip[(me + 1) % K]))
     off = bits(topo.mask(core, cab) & topo.mask(core, sw))
     m_sw, m_cab = off[0::2], off[1::2]
-    dst = lambda d: DstId(rid=topo.addr(d, core)[0], pnc=topo.addr(d, core)[1])
     nloc = [0]
 
     def send(ts):
         for t in ts:
             nloc[0] += len(t[4])
-        g.remote_dma_fused([RemoteDMATransfer(dst_ids=[dst(d)], dma_engine_mask=sum(e), remote_sem=s, src=i, dst=o)
-                            for d, o, i, s, e in ts], local_sem=sem.loc)
+        g.remote_dma_fused([RemoteDMATransfer(dst_ids=[DstId(rid=topo.addr(d, core)[0], pnc=topo.addr(d, core)[1]) for d in ds],
+                                              dma_engine_mask=sum(e), remote_sem=s, srcs=[i], dsts=[o for d in ds])
+                            for ds, o, i, s, e in ts], local_sem=sem.loc)
 
     if mine is not None:
         g.scalar.dma_start(out=T.hrow[0:1, 0:2], in_=T.hh[0:1, 0:2]).then_inc(sem.hl, 16)
@@ -79,93 +85,80 @@ def rank_program(g, core, T, topo):
 
     g.iota(T.pi[:], [[0, 1]], 0, 1).then_inc(sem.gi, 1)
     if mine is not None:
-        g.iota(T.ja[:], [[16, W // 16]], 0, 1).then_inc(sem.gi, 1)
+        g.iota(T.ja[:], [[16, L1]], 0, 1).then_inc(sem.gi, 1)
     g.iota(T.ba[:], [[W, 3], [16, C // 16]], W * r0 + C * me, 1).then_inc(sem.gi, 1)
     g.iota(T.ta[:], [[0, 3], [16, C // 16]], 0, 1).then_inc(sem.gi, 1)
     g.vector.wait_ge(sem.gi, 3 if mine is None else 4)
     nv = [0]
 
-    def vec(call, *a):
-        call(*a).then_inc(sem.v, 1)
-        nv[0] += 1
+    def vec(*calls):
+        for call, *a in calls:
+            call(*a).then_inc(sem.v, 1)
+            nv[0] += 1
         g.vector.wait_ge(sem.v, nv[0])
 
-    vec(g.vector.tensor_scalar, T.pg[:], T.pi[:], 112, None, Op.bitwise_and)
-    vec(g.vector.tensor_copy, T.pf[:], T.pg[:])
+    ts, tt, tc = g.vector.tensor_scalar, g.vector.tensor_tensor, g.vector.tensor_copy
+    vec((ts, T.pg[:], T.pi[:], 112, None, Op.bitwise_and))
+    vec((tc, T.pf[:], T.pg[:]))
     if mine is not None:
-        vec(g.vector.tensor_scalar, T.jb[:], T.ja[:], T.pf[:, 0:1], None, Op.subtract)
-    vec(g.vector.tensor_scalar, T.bb[:], T.ba[:], T.pf[:, 0:1], None, Op.subtract)
-    vec(g.vector.tensor_scalar, T.tb[:], T.ta[:], T.pf[:, 0:1], None, Op.subtract)
+        vec((ts, T.jb[:], T.ja[:], T.pf[:, 0:1], None, Op.subtract))
+    vec((ts, T.bb[:], T.ba[:], T.pf[:, 0:1], None, Op.subtract),
+        (ts, T.tb[:], T.ta[:], T.pf[:, 0:1], None, Op.subtract))
 
-    helpers = [c for c in chip if T.rank_of(c) is None]
-    h_sender = T.cores[ranks[-1]]
     if mine is not None:
         g.wait_ge(sem.hl, 16)
         g.partition_broadcast(T.hb[:], T.hrow[0:1, 0:2], 128).then_inc(sem.gb, 1)
         g.vector.wait_ge(sem.gb, 1)
-        if core == h_sender:
-            g.sync.wait_ge(sem.gb, 1)
-            g.sync.dma_start(out=T.hd[:], in_=T.hb[:]).then_inc(sem.hs, 16)
+        g.wait_ge(sem.gb, 1)
+        send([([c for c in chip if T.rank_of(c) is None][pos::3], T.hb[:], T.hb[:], sem.hr, on)])
     else:
-        g.sync.wait_ge(sem.hr, 1)
-        g.sync.dma_start(out=T.hb[:], in_=T.hd[:]).then_inc(sem.hl, 16)
-        g.vector.wait_ge(sem.hl, 16)
-    vec(g.vector.tensor_copy, T.hf[:], T.hb[:, 0:1])
+        g.vector.wait_ge(sem.hr, len(on))
+    vec((tc, T.hf[:], T.hb[:, 0:1]))
 
-    mycols = lambda r: (r * C, r * C + C)
     if mine is not None:
-        vec(g.vector.tensor_scalar, T.jc[:], T.jb[:], T.hf[:, 0:1], None, Op.add)
-        vec(g.vector.tensor_scalar, T.jd[:], T.jc[:], W - 1, None, Op.bitwise_and)
-        g.vector.tensor_copy(T.off1[:], T.jd[:]).then_inc(sem.l1, 1)
+        vec((ts, T.jc[:], T.jb[:], T.hf[:, 0:1], None, Op.add))
+        vec((ts, T.jd[:], T.jc[:], W - 1, None, Op.bitwise_and))
+        tc(T.off1[:], T.jd[:]).then_inc(sem.l1, 1)
         for q in (g.vector, g.scalar):
             q.wait_ge(sem.l1, 1)
             q.wait_ge(sem.xl, 16)
-        waves = [list(range(0, K, 2)), list(range(1, K, 2))]
-        a0, a1 = mycols(mine)
-        for n, k in enumerate(waves[0] + waves[1]):
+        a0, a1 = mine * C, mine * C + C
+        for k in range(K):
             out = T.tab[:, a0:a1] if k == me else T.rot[:, k * C:k * C + C]
-            s = sem.ro if k == me else sem.ra if k in waves[0] else sem.rb
+            s = sem.ro if k == me else sem.ra if k < K // 2 else sem.rb
             src = T.xs[:, 0:W].indirect(T.off1[:, k * C // 16:(k + 1) * C // 16])
-            if n % 2 == 0:
-                g.vector.tensor_copy(out, src).then_inc(s, 1)
+            if k % 2 == 0:
+                tc(out, src).then_inc(s, 1)
             else:
                 g.scalar.activation(out, src, Act.Copy).then_inc(s, 1)
-        for w, s in zip(waves, (sem.ra, sem.rb)):
-            ks = [k for k in w if k != me]
+        for w, s in ((0, sem.ra), (1, sem.rb)):
+            ks = [k for k in range(w * K // 2, (w + 1) * K // 2) if k != me]
             g.wait_ge(s, len(ks))
-            send([(chip[k], T.tab[:, a0:a1], T.rot[:, k * C:k * C + C], sem.s1b if pos == 2 else sem.s1a, on[n::4])
-                  for n, k in enumerate(ks)])
+            send([([chip[k]], T.tab[:, a0:a1], T.rot[:, k * C:k * C + C], sem.s1b if pos == 2 else sem.s1a, on[k % 4::4])
+                  for k in ks])
         g.wait_ge(sem.ro, 1)
 
-    per = len(on[0::4])
     base = r0 * C
-    chunks = [(0, 2 * C, sem.s1a, sem.ca, per * len([i for i in (0, 1) if i != pos])),
-              (2 * C, 3 * C, sem.s1b, sem.cb, per * len([i for i in (2,) if i != pos]))]
+    chunks = [(0, 2 * C, sem.s1a, sem.ca, 4 * len([i for i in (0, 1) if i != pos])),
+              (2 * C, 3 * C, sem.s1b, sem.cb, 4 * len([i for i in (2,) if i != pos]))]
     for lo, hi, s_in, s_out, n in chunks:
         if n:
             g.wait_ge(s_in, n)
         ap = T.tab[:, base + lo:base + hi]
-        send([(cab, ap, ap, s_out, m_cab), (sw, ap, ap, sem.sw, m_sw)])
-    if core == h_sender:
-        g.wait_ge(sem.hs, 16)
-        e = m_sw[0]
-        nloc[0] += 1
-        g.remote_dma_fused([RemoteDMATransfer(dst_ids=[dst(c) for c in helpers], dma_engine_mask=e, remote_sem=sem.hr,
-                                              srcs=[T.hd[:]], dsts=[T.hd[:] for c in helpers])], local_sem=sem.loc)
-    cbase = first_rank(cab) * C
+        send([([cab], ap, ap, s_out, m_cab), ([sw], ap, ap, sem.sw, m_sw)])
+    cbase = ranks_at(cab_chip)[0] * C
     relay = [m_sw, off]
     for (lo, hi, s_in, s_out, n), e in zip(chunks, relay):
         g.wait_ge(s_out, len(m_cab))
         ap = T.tab[:, cbase + lo:cbase + hi]
-        send([(sw, ap, ap, sem.sw, e)])
+        send([([sw], ap, ap, sem.sw, e)])
 
-    vec(g.vector.tensor_scalar, T.q0[:], T.bb[:], T.hf[:, 0:1], None, Op.add)
-    vec(g.vector.tensor_scalar, T.q1[:], T.q0[:], 11, None, Op.arith_shift_right)
-    vec(g.vector.tensor_scalar, T.q2[:], T.q1[:], N, -N * C, Op.is_ge, Op.mult)
-    vec(g.vector.tensor_scalar, T.q3[:], T.q1[:], C, None, Op.mult)
-    vec(g.vector.tensor_tensor, T.q4[:], T.q3[:], T.q2[:], Op.add)
-    vec(g.vector.tensor_tensor, T.q5[:], T.q4[:], T.tb[:], Op.add)
-    g.vector.tensor_copy(T.off2[:], T.q5[:]).then_inc(sem.l2, 1)
+    vec((ts, T.q0[:], T.bb[:], T.hf[:, 0:1], None, Op.add))
+    vec((ts, T.q1[:], T.q0[:], 3, 0x3F00, Op.arith_shift_right, Op.bitwise_and),
+        (ts, T.q2[:], T.q0[:], N * W, -N * C, Op.is_ge, Op.mult))
+    vec((tt, T.q3[:], T.q1[:], T.tb[:], Op.add))
+    vec((tt, T.q4[:], T.q3[:], T.q2[:], Op.add))
+    tc(T.off2[:], T.q4[:]).then_inc(sem.l2, 1)
     nsw = 2 * len(m_sw) + len(relay[0]) + len(relay[1])
     for q in (g.vector, g.scalar):
         q.wait_ge(sem.l2, 1)
@@ -182,7 +175,7 @@ def rank_program(g, core, T, topo):
         out, s = (T.fin[:, me * C + lo:me * C + hi], sem.so) if i == pos else (T.sel[:, i * C + lo:i * C + hi], sem.sl)
         src = T.tab[:, 0:N * C].indirect(T.off2[:, (i * C + lo) // 16:(i * C + hi) // 16])
         if q == 0:
-            g.vector.tensor_copy(out, src).then_inc(s, 1)
+            tc(out, src).then_inc(s, 1)
         else:
             g.scalar.activation(out, src, Act.Copy).then_inc(s, 1)
 
@@ -191,16 +184,18 @@ def rank_program(g, core, T, topo):
     for q in (0, 1):
         pick(q, ends[q], 0, C)
         pick(q, mid, q * C // 2, (q + 1) * C // 2)
-    targets = [i for i in range(3) if i != pos]
+    dies = [topo.die(T.cores[r]) for r in ranks]
+    major = max(dies, key=dies.count)
+    same = [i for i in range(3) if dies[i] == major]
+    lane = {i: 2 * same.index(i) if i in same else 1 for i in range(3)}
     g.wait_ge(sem.sl, 4 if pos is None else 2)
-    fe = lambda k: 2 if T.rank_of(chip[k]) is None else 4
-    send([(T.cores[r0 + i], T.fin[:, me * C:me * C + C], T.sel[:, i * C:i * C + C], sem.fin0 if me < K // 2 else sem.fin1,
-           off[n * fe(me):(n + 1) * fe(me)]) for n, i in enumerate(targets)])
+    send([([T.cores[r0 + i]], T.fin[:, me * C:me * C + C], T.sel[:, i * C:i * C + C], sem.fin0 if me < K // 2 else sem.fin1,
+           on[lane[i]::4]) for i in range(3) if i != pos])
 
     if mine is not None:
         for half, (q, s) in enumerate(((g.sync, sem.fin0), (g.scalar, sem.fin1))):
             ks = list(range(half * K // 2, (half + 1) * K // 2))
-            q.wait_ge(s, sum([fe(k) for k in ks if k != me]))
+            q.wait_ge(s, 4 * len([k for k in ks if k != me]))
             if me in ks:
                 q.wait_ge(sem.so, 2)
             q.dma_start(out=T.y[:, half * W // 2:(half + 1) * W // 2],

@@ -3,41 +3,33 @@ from concourse.mybir import AluOpType as Op, ActivationFunctionType as Act
 
 WORLD = 512
 N, W = 12, 2048
+H = N // 2
 K = 8
 C = W // K
-L1, L2 = W // 16, 3 * C // 16
+G = C // 16
+L1, L2 = W // 16, 6 * G
+KIND = "PR"
 
 SCRATCH = {
     "xs": ("sbuf", [128, W], "bfloat16"),
-    "rot": ("sbuf", [128, W], "bfloat16"),
-    "tab": ("sbuf", [128, N * C], "bfloat16"),
-    "sel": ("sbuf", [128, 3 * C], "bfloat16"),
-    "fin": ("sbuf", [128, W], "bfloat16"),
+    "tab": ("sbuf", [128, H * C], "bfloat16"),
+    "sel": ("sbuf", [128, 6 * C], "bfloat16"),
+    "fin": ("sbuf", [128, 2 * W], "bfloat16"),
+    "out": ("sbuf", [128, W], "bfloat16"),
     "hrow": ("sbuf", [1, 2], "int32"),
     "hb": ("sbuf", [128, 2], "int32"),
     "hf": ("sbuf", [128, 1], "float32"),
     "pi": ("sbuf", [128, 1], "int32"),
     "pg": ("sbuf", [128, 1], "int32"),
     "pf": ("sbuf", [128, 1], "float32"),
-    "ja": ("sbuf", [128, L1], "int32"),
-    "jb": ("sbuf", [128, L1], "int32"),
-    "jc": ("sbuf", [128, L1], "int32"),
-    "jd": ("sbuf", [128, L1], "int32"),
     "off1": ("sbuf", [128, L1], "uint16"),
-    "ba": ("sbuf", [128, L2], "int32"),
-    "bb": ("sbuf", [128, L2], "int32"),
-    "ta": ("sbuf", [128, L2], "int32"),
-    "tb": ("sbuf", [128, L2], "int32"),
-    "q0": ("sbuf", [128, L2], "int32"),
-    "q1": ("sbuf", [128, L2], "int32"),
-    "q2": ("sbuf", [128, L2], "int32"),
-    "q3": ("sbuf", [128, L2], "int32"),
-    "q4": ("sbuf", [128, L2], "int32"),
-    "q5": ("sbuf", [128, L2], "int32"),
     "off2": ("sbuf", [128, L2], "uint16"),
 }
-SEMAPHORES = ["xl", "hl", "hr", "gi", "gb", "v", "l1", "l2", "ra", "rb", "ro", "s1a", "s1b", "ca", "cb", "sw",
-              "sl", "so", "fin0", "fin1", "st", "loc"]
+for _n in ("ja", "jb", "jc", "jd", "je", "jf", "jg", "jh", "ji", "jj", "jk"):
+    SCRATCH[_n] = ("sbuf", [128, L1], "int32")
+for _n in ("ba", "bb", "ta", "tb", "q0", "q1", "q2", "q3", "q4", "q5"):
+    SCRATCH[_n] = ("sbuf", [128, L2], "int32")
+SEMAPHORES = ["xl", "hl", "hr", "gi", "gb", "cn", "v", "s1", "ro", "ph", "sa", "sb", "sc", "so", "fin", "mg0", "mg1", "st", "loc"]
 
 
 def bits(m):
@@ -61,16 +53,28 @@ def rank_program(g, core, T, topo):
     sw_chip = order(on_chip([d for d in other if topo.same_plane(core, d)][0]))
     cab_chip = order(on_chip([d for d in other if topo.rack(topo.host(d)) != topo.rack(topo.host(core))
                               and topo.may_write(core, d)][0]))
-    sw, cab = sw_chip[me], cab_chip[me]
     ranks_at = lambda cs: sorted([T.rank_of(c) for c in cs if T.rank_of(c) is not None])
     ranks = ranks_at(chip)
     r0 = ranks[0]
     mine = T.rank_of(core)
     pos = None if mine is None else mine - r0
+    helpers = [c for c in chip if T.rank_of(c) is None]
     on = bits(topo.mask(core, chip[(me + 1) % K]))
-    off = bits(topo.mask(core, cab) & topo.mask(core, sw))
-    m_sw, m_cab = off[0::2], off[1::2]
+    off = bits(topo.mask(core, cab_chip[me]) & topo.mask(core, sw_chip[me]))
+    rest = [e for e in on if e not in off]
     nloc = [0]
+
+    def start(cs):
+        both = ranks + ranks_at(cs)
+        return [r for r in both if (r - 1) % N not in both][0]
+
+    first = {"P": sw_chip, "R": cab_chip}
+    last = {"P": cab_chip, "R": sw_chip}
+    kind = lambda m: KIND[m // (K // 2)]
+    b = start(first[kind(me)])
+    own = (r0 - b) % N
+    far0 = ranks_at(last[kind(me)])[0]
+    far = (far0 - b) % N
 
     def send(ts):
         for t in ts:
@@ -79,16 +83,6 @@ def rank_program(g, core, T, topo):
                                               dma_engine_mask=sum(e), remote_sem=s, srcs=[i], dsts=[o for d in ds])
                             for ds, o, i, s, e in ts], local_sem=sem.loc)
 
-    if mine is not None:
-        g.scalar.dma_start(out=T.hrow[0:1, 0:2], in_=T.hh[0:1, 0:2]).then_inc(sem.hl, 16)
-        g.sync.dma_start(out=T.xs[:], in_=T.x[:]).then_inc(sem.xl, 16)
-
-    g.iota(T.pi[:], [[0, 1]], 0, 1).then_inc(sem.gi, 1)
-    if mine is not None:
-        g.iota(T.ja[:], [[16, L1]], 0, 1).then_inc(sem.gi, 1)
-    g.iota(T.ba[:], [[W, 3], [16, C // 16]], W * r0 + C * me, 1).then_inc(sem.gi, 1)
-    g.iota(T.ta[:], [[0, 3], [16, C // 16]], 0, 1).then_inc(sem.gi, 1)
-    g.vector.wait_ge(sem.gi, 3 if mine is None else 4)
     nv = [0]
 
     def vec(*calls):
@@ -98,107 +92,141 @@ def rank_program(g, core, T, topo):
         g.vector.wait_ge(sem.v, nv[0])
 
     ts, tt, tc = g.vector.tensor_scalar, g.vector.tensor_tensor, g.vector.tensor_copy
+
+    if mine is not None:
+        g.scalar.dma_start(out=T.hrow[0:1, 0:2], in_=T.hh[0:1, 0:2]).then_inc(sem.hl, 16)
+        g.sync.dma_start(out=T.xs[:], in_=T.x[:]).then_inc(sem.xl, 16)
+
+    if mine is not None:
+        g.iota(T.ta[:], [[0, 6], [16, G]], 0, 1).then_inc(sem.gi, 1)
+        g.wait_ge(sem.gi, 1)
+        send([(helpers[pos::3], T.ta[:], T.ta[:], sem.cn, on)])
+    else:
+        i = helpers.index(core)
+        half = i % 2
+        peers = list(range(half, len(helpers), 2))
+        cols = slice(half * L1 // 2, (half + 1) * L1 // 2)
+        g.iota(T.ja[:, cols], [[16, L1 // 2]], half * W // 2, 1).then_inc(sem.gi, 1)
+        g.wait_ge(sem.gi, 1)
+        send([([T.cores[r] for r in ranks if peers[(r - r0) % len(peers)] == i], T.ja[:, cols], T.ja[:, cols], sem.cn, on)])
+
+    if mine is not None:
+        g.wait_ge(sem.xl, 16)
+        slot = lambda k: (mine - start(first[kind(k)])) % N * C
+        for w in (0, 1):
+            send([([chip[k]], T.tab[:, slot(k):slot(k) + C], T.xs[:, k * C:k * C + C], sem.s1, on[k % 4::4])
+                  for k in range(w * K // 2, (w + 1) * K // 2) if k != me])
+
+    g.iota(T.pi[:], [[0, 1]], 0, 1).then_inc(sem.gi, 1)
+    g.iota(T.ba[:], [[W * (own - far), 2], [W, 3], [-16, G]], W * far + W - 1 - C * me, -1).then_inc(sem.gi, 1)
+    g.vector.wait_ge(sem.gi, 3)
     vec((ts, T.pg[:], T.pi[:], 112, None, Op.bitwise_and))
     vec((tc, T.pf[:], T.pg[:]))
+    vec((ts, T.bb[:], T.ba[:], T.pf[:, 0:1], None, Op.add))
     if mine is not None:
+        vec((ts, T.tb[:], T.ta[:], T.pf[:, 0:1], None, Op.subtract))
+        g.vector.wait_ge(sem.cn, 2 * len(on))
         vec((ts, T.jb[:], T.ja[:], T.pf[:, 0:1], None, Op.subtract))
-    vec((ts, T.bb[:], T.ba[:], T.pf[:, 0:1], None, Op.subtract),
-        (ts, T.tb[:], T.ta[:], T.pf[:, 0:1], None, Op.subtract))
+    else:
+        g.vector.wait_ge(sem.cn, len(on))
+        vec((ts, T.tb[:], T.ta[:], T.pf[:, 0:1], None, Op.subtract))
 
     if mine is not None:
         g.wait_ge(sem.hl, 16)
         g.partition_broadcast(T.hb[:], T.hrow[0:1, 0:2], 128).then_inc(sem.gb, 1)
         g.vector.wait_ge(sem.gb, 1)
         g.wait_ge(sem.gb, 1)
-        send([([c for c in chip if T.rank_of(c) is None][pos::3], T.hb[:], T.hb[:], sem.hr, on)])
+        send([(helpers[pos::3], T.hb[:], T.hb[:], sem.hr, on)])
+        g.scalar.wait_ge(sem.xl, 16)
+        g.scalar.activation(T.tab[:, slot(me):slot(me) + C], T.xs[:, me * C:me * C + C], Act.Copy).then_inc(sem.ro, 1)
+        g.wait_ge(sem.ro, 1)
     else:
         g.vector.wait_ge(sem.hr, len(on))
     vec((tc, T.hf[:], T.hb[:, 0:1]))
 
-    if mine is not None:
-        vec((ts, T.jc[:], T.jb[:], T.hf[:, 0:1], None, Op.add))
-        vec((ts, T.jd[:], T.jc[:], W - 1, None, Op.bitwise_and))
-        tc(T.off1[:], T.jd[:]).then_inc(sem.l1, 1)
-        for q in (g.vector, g.scalar):
-            q.wait_ge(sem.l1, 1)
-            q.wait_ge(sem.xl, 16)
-        a0, a1 = mine * C, mine * C + C
-        for k in range(K):
-            out = T.tab[:, a0:a1] if k == me else T.rot[:, k * C:k * C + C]
-            s = sem.ro if k == me else sem.ra if k < K // 2 else sem.rb
-            src = T.xs[:, 0:W].indirect(T.off1[:, k * C // 16:(k + 1) * C // 16])
-            if k % 2 == 0:
-                tc(out, src).then_inc(s, 1)
-            else:
-                g.scalar.activation(out, src, Act.Copy).then_inc(s, 1)
-        for w, s in ((0, sem.ra), (1, sem.rb)):
-            ks = [k for k in range(w * K // 2, (w + 1) * K // 2) if k != me]
-            g.wait_ge(s, len(ks))
-            send([([chip[k]], T.tab[:, a0:a1], T.rot[:, k * C:k * C + C], sem.s1b if pos == 2 else sem.s1a, on[k % 4::4])
-                  for k in ks])
-        g.wait_ge(sem.ro, 1)
-
-    base = r0 * C
-    chunks = [(0, 2 * C, sem.s1a, sem.ca, 4 * len([i for i in (0, 1) if i != pos])),
-              (2 * C, 3 * C, sem.s1b, sem.cb, 4 * len([i for i in (2,) if i != pos]))]
-    for lo, hi, s_in, s_out, n in chunks:
-        if n:
-            g.wait_ge(s_in, n)
-        ap = T.tab[:, base + lo:base + hi]
-        send([([cab], ap, ap, s_out, m_cab), ([sw], ap, ap, sem.sw, m_sw)])
-    cbase = ranks_at(cab_chip)[0] * C
-    relay = [m_sw, off]
-    for (lo, hi, s_in, s_out, n), e in zip(chunks, relay):
-        g.wait_ge(s_out, len(m_cab))
-        ap = T.tab[:, cbase + lo:cbase + hi]
-        send([([sw], ap, ap, sem.sw, e)])
+    n1 = 4 * len([i for i in range(3) if i != pos])
+    g.wait_ge(sem.s1, n1)
+    ap = T.tab[:, own * C:(own + 3) * C]
+    send([([first[kind(me)][me]], ap, ap, sem.ph, off)])
 
     vec((ts, T.q0[:], T.bb[:], T.hf[:, 0:1], None, Op.add))
     vec((ts, T.q1[:], T.q0[:], 3, 0x3F00, Op.arith_shift_right, Op.bitwise_and),
         (ts, T.q2[:], T.q0[:], N * W, -N * C, Op.is_ge, Op.mult))
-    vec((tt, T.q3[:], T.q1[:], T.tb[:], Op.add))
-    vec((tt, T.q4[:], T.q3[:], T.q2[:], Op.add))
-    tc(T.off2[:], T.q4[:]).then_inc(sem.l2, 1)
-    nsw = 2 * len(m_sw) + len(relay[0]) + len(relay[1])
+    vec((tt, T.q3[:], T.q1[:], T.q2[:], Op.add))
+    vec((ts, T.q4[:], T.q3[:], (H - 1) * C, None, Op.min))
+    vec((tt, T.q5[:], T.q4[:], T.tb[:], Op.add))
+    vec((tc, T.off2[:], T.q5[:]))
+    if mine is not None:
+        bP, bR = [(mine - start(first[k])) % N for k in KIND]
+        vec((ts, T.jc[:], T.jb[:], T.hf[:, 0:1], None, Op.add))
+        vec((ts, T.jd[:], T.jc[:], W - 1, None, Op.bitwise_and),
+            (ts, T.je[:], T.jc[:], W // 2, None, Op.bitwise_and))
+        vec((ts, T.jf[:], T.je[:], 2 * (bR - bP), bP * W, Op.mult, Op.add))
+        vec((tt, T.jg[:], T.jf[:], T.jc[:], Op.add))
+        vec((ts, T.jh[:], T.jg[:], N * W, -N * W, Op.is_ge, Op.mult))
+        vec((tt, T.ji[:], T.jg[:], T.jh[:], Op.add))
+        vec((ts, T.jj[:], T.ji[:], H * W, W, Op.is_ge, Op.mult))
+        vec((tt, T.jk[:], T.jj[:], T.jd[:], Op.add))
+        vec((tc, T.off1[:], T.jk[:]))
+    g.scalar.wait_ge(sem.v, nv[0])
     for q in (g.vector, g.scalar):
-        q.wait_ge(sem.l2, 1)
-        q.wait_ge(sem.sw, nsw)
-        q.wait_ge(sem.ca, len(m_cab))
-        q.wait_ge(sem.cb, len(m_cab))
+        q.wait_ge(sem.ph, len(off))
+        q.wait_ge(sem.s1, n1)
         if mine is not None:
             q.wait_ge(sem.ro, 1)
-        for lo, hi, s_in, s_out, n in chunks:
-            if n:
-                q.wait_ge(s_in, n)
 
     def pick(q, i, lo, hi):
-        out, s = (T.fin[:, me * C + lo:me * C + hi], sem.so) if i == pos else (T.sel[:, i * C + lo:i * C + hi], sem.sl)
-        src = T.tab[:, 0:N * C].indirect(T.off2[:, (i * C + lo) // 16:(i * C + hi) // 16])
+        if pos is not None and i == 3 + pos:
+            out, s = T.fin[:, me * C + lo:me * C + hi], sem.so
+        else:
+            out, s = T.sel[:, i * C + lo:i * C + hi], sem.sa if i < 2 else sem.sb if i < 3 else sem.sc
+        src = T.tab[:, 0:H * C].indirect(T.off2[:, (i * C + lo) // 16:(i * C + hi) // 16])
         if q == 0:
             tc(out, src).then_inc(s, 1)
         else:
             g.scalar.activation(out, src, Act.Copy).then_inc(s, 1)
 
-    mid = 1 if pos is None else pos
-    ends = [i for i in range(3) if i != mid]
-    for q in (0, 1):
-        pick(q, ends[q], 0, C)
-        pick(q, mid, q * C // 2, (q + 1) * C // 2)
-    dies = [topo.die(T.cores[r]) for r in ranks]
-    major = max(dies, key=dies.count)
-    same = [i for i in range(3) if dies[i] == major]
-    lane = {i: 2 * same.index(i) if i in same else 1 for i in range(3)}
-    g.wait_ge(sem.sl, 4 if pos is None else 2)
-    send([([T.cores[r0 + i]], T.fin[:, me * C:me * C + C], T.sel[:, i * C:i * C + C], sem.fin0 if me < K // 2 else sem.fin1,
-           on[lane[i]::4]) for i in range(3) if i != pos])
+    mid = 4 if pos is None else 3 + pos
+    for x, y, z in ((0, 1, 2), [i for i in (3, 4, 5) if i != mid] + [mid]):
+        pick(0, x, 0, C)
+        pick(1, y, 0, C)
+        for q in (0, 1):
+            pick(q, z, q * C // 2, (q + 1) * C // 2)
+    fb, nb = W + me * C, me * C
+    far_t = [([T.cores[far0 + i]], T.fin[:, fb:fb + C], T.sel[:, i * C:i * C + C], sem.fin, e)
+             for i, e in enumerate((off[0::2], off[1::2], off))]
+    near = [i for i in range(3) if i != pos]
+    near_t = [([T.cores[r0 + i]], T.fin[:, nb:nb + C], T.sel[:, (3 + i) * C:(4 + i) * C], sem.fin, e)
+              for i, e in zip(near, (rest[0::2], rest[1::2], rest))]
+    g.wait_ge(sem.sa, 2)
+    send(far_t[0:2])
+    g.wait_ge(sem.sb, 2)
+    send(far_t[2:3])
+    g.wait_ge(sem.sc, 4 if pos is None else 2)
+    send(near_t[0:2])
+    if pos is None:
+        send(near_t[2:3])
 
     if mine is not None:
-        for half, (q, s) in enumerate(((g.sync, sem.fin0), (g.scalar, sem.fin1))):
-            ks = list(range(half * K // 2, (half + 1) * K // 2))
-            q.wait_ge(s, 4 * len([k for k in ks if k != me]))
-            if me in ks:
-                q.wait_ge(sem.so, 2)
+        nf = 0
+        for d in range(K):
+            nf += (4, 4, 8)[pos]
+            if d != me:
+                nf += (4, 4, 8)[pos] if T.rank_of(chip[d]) is None else 4
+        for q in (g.vector, g.scalar):
+            q.wait_ge(sem.fin, nf)
+            q.wait_ge(sem.so, 2)
+        for k in range(4):
+            lo, hi = k * W // 4, (k + 1) * W // 4
+            s = sem.mg0 if k < 2 else sem.mg1
+            src = T.fin[:, 0:2 * W].indirect(T.off1[:, lo // 16:hi // 16])
+            if k % 2 == 0:
+                tc(T.out[:, lo:hi], src).then_inc(s, 1)
+            else:
+                g.scalar.activation(T.out[:, lo:hi], src, Act.Copy).then_inc(s, 1)
+        for half, (q, s) in enumerate(((g.sync, sem.mg0), (g.scalar, sem.mg1))):
+            q.wait_ge(s, 2)
             q.dma_start(out=T.y[:, half * W // 2:(half + 1) * W // 2],
-                        in_=T.fin[:, half * W // 2:(half + 1) * W // 2]).then_inc(sem.st, 16)
+                        in_=T.out[:, half * W // 2:(half + 1) * W // 2]).then_inc(sem.st, 16)
         g.wait_ge(sem.st, 32)
     g.wait_ge(sem.loc, nloc[0])

from concourse.bass import DstId, RemoteDMATransfer
from concourse.mybir import AluOpType as Op, ActivationFunctionType as Act

WORLD = 512
N, W = 12, 2048
H = N // 2
K = 8
C = W // K
G = C // 16
L1, L2 = W // 16, 6 * G
KIND = "PR"

SCRATCH = {
    "xs": ("sbuf", [128, W], "bfloat16"),
    "tab": ("sbuf", [128, H * C], "bfloat16"),
    "sel": ("sbuf", [128, 6 * C], "bfloat16"),
    "fin": ("sbuf", [128, 2 * W], "bfloat16"),
    "out": ("sbuf", [128, W], "bfloat16"),
    "hrow": ("sbuf", [1, 2], "int32"),
    "hb": ("sbuf", [128, 2], "int32"),
    "hf": ("sbuf", [128, 1], "float32"),
    "pi": ("sbuf", [128, 1], "int32"),
    "pg": ("sbuf", [128, 1], "int32"),
    "pf": ("sbuf", [128, 1], "float32"),
    "off1": ("sbuf", [128, L1], "uint16"),
    "off2": ("sbuf", [128, L2], "uint16"),
}
for _n in ("ja", "jb", "jc", "jd", "je", "jf", "jg", "jh", "ji", "jj", "jk"):
    SCRATCH[_n] = ("sbuf", [128, L1], "int32")
for _n in ("ba", "bb", "ta", "tb", "q0", "q1", "q2", "q3", "q4", "q5"):
    SCRATCH[_n] = ("sbuf", [128, L2], "int32")
SEMAPHORES = ["xl", "hl", "hr", "gi", "gb", "cn", "v", "s1", "ro", "ph", "sa", "sb", "sc", "so", "fin", "mg0", "mg1", "st", "loc"]


def bits(m):
    return [1 << i for i in range(16) if (m >> i) & 1]


def rank_program(g, core, T, topo):
    sem = T.sem
    place = lambda c: (topo.host(c), topo.chip(c))
    if place(core) not in [place(c) for c in T.cores]:
        return
    on_chip = lambda c: [d for d in range(WORLD) if place(d) == place(c)]

    def order(cs):
        a, b = [[c for c in cs if topo.die(c) == topo.die(e)] for e in (cs[0], cs[-1])]
        return [c for i in (0, 2, 1, 3) for c in (a[i], b[i])]

    chip = order(on_chip(core))
    me = chip.index(core)
    other = [d for d in T.cores if place(d) != place(core)]
    sw_chip = order(on_chip([d for d in other if topo.same_plane(core, d)][0]))
    cab_chip = order(on_chip([d for d in other if topo.rack(topo.host(d)) != topo.rack(topo.host(core))
                              and topo.may_write(core, d)][0]))
    ranks_at = lambda cs: sorted([T.rank_of(c) for c in cs if T.rank_of(c) is not None])
    ranks = ranks_at(chip)
    r0 = ranks[0]
    mine = T.rank_of(core)
    pos = None if mine is None else mine - r0
    helpers = [c for c in chip if T.rank_of(c) is None]
    on = bits(topo.mask(core, chip[(me + 1) % K]))
    off = bits(topo.mask(core, cab_chip[me]) & topo.mask(core, sw_chip[me]))
    rest = [e for e in on if e not in off]
    nloc = [0]

    def start(cs):
        both = ranks + ranks_at(cs)
        return [r for r in both if (r - 1) % N not in both][0]

    first = {"P": sw_chip, "R": cab_chip}
    last = {"P": cab_chip, "R": sw_chip}
    kind = lambda m: KIND[m // (K // 2)]
    b = start(first[kind(me)])
    own = (r0 - b) % N
    far0 = ranks_at(last[kind(me)])[0]
    far = (far0 - b) % N

    def send(ts):
        for t in ts:
            nloc[0] += len(t[4])
        g.remote_dma_fused([RemoteDMATransfer(dst_ids=[DstId(rid=topo.addr(d, core)[0], pnc=topo.addr(d, core)[1]) for d in ds],
                                              dma_engine_mask=sum(e), remote_sem=s, srcs=[i], dsts=[o for d in ds])
                            for ds, o, i, s, e in ts], local_sem=sem.loc)

    nv = [0]

    def vec(*calls):
        for call, *a in calls:
            call(*a).then_inc(sem.v, 1)
            nv[0] += 1
        g.vector.wait_ge(sem.v, nv[0])

    ts, tt, tc = g.vector.tensor_scalar, g.vector.tensor_tensor, g.vector.tensor_copy

    if mine is not None:
        g.scalar.dma_start(out=T.hrow[0:1, 0:2], in_=T.hh[0:1, 0:2]).then_inc(sem.hl, 16)
        g.sync.dma_start(out=T.xs[:], in_=T.x[:]).then_inc(sem.xl, 16)

    if mine is not None:
        g.iota(T.ta[:], [[0, 6], [16, G]], 0, 1).then_inc(sem.gi, 1)
        g.wait_ge(sem.gi, 1)
        send([(helpers[pos::3], T.ta[:], T.ta[:], sem.cn, on)])
    else:
        i = helpers.index(core)
        half = i % 2
        peers = list(range(half, len(helpers), 2))
        cols = slice(half * L1 // 2, (half + 1) * L1 // 2)
        g.iota(T.ja[:, cols], [[16, L1 // 2]], half * W // 2, 1).then_inc(sem.gi, 1)
        g.wait_ge(sem.gi, 1)
        send([([T.cores[r] for r in ranks if peers[(r - r0) % len(peers)] == i], T.ja[:, cols], T.ja[:, cols], sem.cn, on)])

    if mine is not None:
        g.wait_ge(sem.xl, 16)
        slot = lambda k: (mine - start(first[kind(k)])) % N * C
        for w in (0, 1):
            send([([chip[k]], T.tab[:, slot(k):slot(k) + C], T.xs[:, k * C:k * C + C], sem.s1, on[k % 4::4])
                  for k in range(w * K // 2, (w + 1) * K // 2) if k != me])

    g.iota(T.pi[:], [[0, 1]], 0, 1).then_inc(sem.gi, 1)
    g.iota(T.ba[:], [[W * (own - far), 2], [W, 3], [-16, G]], W * far + W - 1 - C * me, -1).then_inc(sem.gi, 1)
    g.vector.wait_ge(sem.gi, 3)
    vec((ts, T.pg[:], T.pi[:], 112, None, Op.bitwise_and))
    vec((tc, T.pf[:], T.pg[:]))
    vec((ts, T.bb[:], T.ba[:], T.pf[:, 0:1], None, Op.add))
    if mine is not None:
        vec((ts, T.tb[:], T.ta[:], T.pf[:, 0:1], None, Op.subtract))
        g.vector.wait_ge(sem.cn, 2 * len(on))
        vec((ts, T.jb[:], T.ja[:], T.pf[:, 0:1], None, Op.subtract))
    else:
        g.vector.wait_ge(sem.cn, len(on))
        vec((ts, T.tb[:], T.ta[:], T.pf[:, 0:1], None, Op.subtract))

    if mine is not None:
        g.wait_ge(sem.hl, 16)
        g.partition_broadcast(T.hb[:], T.hrow[0:1, 0:2], 128).then_inc(sem.gb, 1)
        g.vector.wait_ge(sem.gb, 1)
        g.wait_ge(sem.gb, 1)
        send([(helpers[pos::3], T.hb[:], T.hb[:], sem.hr, on)])
        g.scalar.wait_ge(sem.xl, 16)
        g.scalar.activation(T.tab[:, slot(me):slot(me) + C], T.xs[:, me * C:me * C + C], Act.Copy).then_inc(sem.ro, 1)
        g.wait_ge(sem.ro, 1)
    else:
        g.vector.wait_ge(sem.hr, len(on))
    vec((tc, T.hf[:], T.hb[:, 0:1]))

    n1 = 4 * len([i for i in range(3) if i != pos])
    g.wait_ge(sem.s1, n1)
    ap = T.tab[:, own * C:(own + 3) * C]
    send([([first[kind(me)][me]], ap, ap, sem.ph, off)])

    vec((ts, T.q0[:], T.bb[:], T.hf[:, 0:1], None, Op.add))
    vec((ts, T.q1[:], T.q0[:], 3, 0x3F00, Op.arith_shift_right, Op.bitwise_and),
        (ts, T.q2[:], T.q0[:], N * W, -N * C, Op.is_ge, Op.mult))
    vec((tt, T.q3[:], T.q1[:], T.q2[:], Op.add))
    vec((ts, T.q4[:], T.q3[:], (H - 1) * C, None, Op.min))
    vec((tt, T.q5[:], T.q4[:], T.tb[:], Op.add))
    vec((tc, T.off2[:], T.q5[:]))
    if mine is not None:
        bP, bR = [(mine - start(first[k])) % N for k in KIND]
        vec((ts, T.jc[:], T.jb[:], T.hf[:, 0:1], None, Op.add))
        vec((ts, T.jd[:], T.jc[:], W - 1, None, Op.bitwise_and),
            (ts, T.je[:], T.jc[:], W // 2, None, Op.bitwise_and))
        vec((ts, T.jf[:], T.je[:], 2 * (bR - bP), bP * W, Op.mult, Op.add))
        vec((tt, T.jg[:], T.jf[:], T.jc[:], Op.add))
        vec((ts, T.jh[:], T.jg[:], N * W, -N * W, Op.is_ge, Op.mult))
        vec((tt, T.ji[:], T.jg[:], T.jh[:], Op.add))
        vec((ts, T.jj[:], T.ji[:], H * W, W, Op.is_ge, Op.mult))
        vec((tt, T.jk[:], T.jj[:], T.jd[:], Op.add))
        vec((tc, T.off1[:], T.jk[:]))
    g.scalar.wait_ge(sem.v, nv[0])
    for q in (g.vector, g.scalar):
        q.wait_ge(sem.ph, len(off))
        q.wait_ge(sem.s1, n1)
        if mine is not None:
            q.wait_ge(sem.ro, 1)

    def pick(q, i, lo, hi):
        if pos is not None and i == 3 + pos:
            out, s = T.fin[:, me * C + lo:me * C + hi], sem.so
        else:
            out, s = T.sel[:, i * C + lo:i * C + hi], sem.sa if i < 2 else sem.sb if i < 3 else sem.sc
        src = T.tab[:, 0:H * C].indirect(T.off2[:, (i * C + lo) // 16:(i * C + hi) // 16])
        if q == 0:
            tc(out, src).then_inc(s, 1)
        else:
            g.scalar.activation(out, src, Act.Copy).then_inc(s, 1)

    mid = 4 if pos is None else 3 + pos
    for x, y, z in ((0, 1, 2), [i for i in (3, 4, 5) if i != mid] + [mid]):
        pick(0, x, 0, C)
        pick(1, y, 0, C)
        for q in (0, 1):
            pick(q, z, q * C // 2, (q + 1) * C // 2)
    fb, nb = W + me * C, me * C
    far_t = [([T.cores[far0 + i]], T.fin[:, fb:fb + C], T.sel[:, i * C:i * C + C], sem.fin, e)
             for i, e in enumerate((off[0::2], off[1::2], off))]
    near = [i for i in range(3) if i != pos]
    near_t = [([T.cores[r0 + i]], T.fin[:, nb:nb + C], T.sel[:, (3 + i) * C:(4 + i) * C], sem.fin, e)
              for i, e in zip(near, (rest[0::2], rest[1::2], rest))]
    g.wait_ge(sem.sa, 2)
    send(far_t[0:2])
    g.wait_ge(sem.sb, 2)
    send(far_t[2:3])
    g.wait_ge(sem.sc, 4 if pos is None else 2)
    send(near_t[0:2])
    if pos is None:
        send(near_t[2:3])

    if mine is not None:
        nf = 0
        for d in range(K):
            nf += (4, 4, 8)[pos]
            if d != me:
                nf += (4, 4, 8)[pos] if T.rank_of(chip[d]) is None else 4
        for q in (g.vector, g.scalar):
            q.wait_ge(sem.fin, nf)
            q.wait_ge(sem.so, 2)
        for k in range(4):
            lo, hi = k * W // 4, (k + 1) * W // 4
            s = sem.mg0 if k < 2 else sem.mg1
            src = T.fin[:, 0:2 * W].indirect(T.off1[:, lo // 16:hi // 16])
            if k % 2 == 0:
                tc(T.out[:, lo:hi], src).then_inc(s, 1)
            else:
                g.scalar.activation(T.out[:, lo:hi], src, Act.Copy).then_inc(s, 1)
        for half, (q, s) in enumerate(((g.sync, sem.mg0), (g.scalar, sem.mg1))):
            q.wait_ge(s, 2)
            q.dma_start(out=T.y[:, half * W // 2:(half + 1) * W // 2],
                        in_=T.out[:, half * W // 2:(half + 1) * W // 2]).then_inc(sem.st, 16)
        g.wait_ge(sem.st, 32)
    g.wait_ge(sem.loc, nloc[0])
